import numpy as np
import ml_dtypes


def mxq(x, axis, fmt="e4m3"):
    dtype, down = {"e4m3": (ml_dtypes.float8_e4m3fn, 7), "e5m2": (ml_dtypes.float8_e5m2, 14)}[fmt]
    v = np.moveaxis(np.asarray(x, np.float32).astype(ml_dtypes.bfloat16).astype(np.float64), axis, -1)
    blocks = v.reshape(v.shape[:-1] + (-1, 32))
    amax = np.abs(blocks).max(-1, keepdims=True)
    byte = np.maximum(np.where(amax > 0, np.frexp(amax)[1] - 1 + 127, 0) - down, 1)
    scale = np.exp2(byte - 127.0)
    codes = (blocks / scale).astype(np.float32).astype(dtype).astype(np.float64)
    return np.moveaxis((codes * scale).reshape(v.shape), -1, axis)


WIDE = False


def mx_kscale(k, group=512):
    if not WIDE:
        return np.ones(k)
    levels = np.array([10, -10, 5, -5, 0])
    if group != 512:
        return np.exp2(np.random.permutation(np.resize(levels, k // group))).repeat(group)
    if k % 512:
        return np.exp2(np.random.permutation(np.resize(levels, k // 32))).repeat(32)
    a = np.empty((k // 512, 16))
    for p in range(k // 512):
        a[p, :8] = np.random.permutation(np.resize(levels, 8))
        for g in range(8):
            far = levels[np.abs(levels - a[p, g]) >= 10]
            a[p, g + 8] = far[np.random.randint(len(far))]
    return np.exp2(a.ravel()).repeat(32)


def f64(x):
    return np.asarray(x).astype(np.float64)


def gelu(v):
    return 0.5 * v * (1.0 + np.tanh(0.7978845608028654 * (v + 0.044715 * v ** 3)))


G, D, M, N = 2, 256, 256, 1024


def setup_inputs():
    n = np.random.standard_normal
    s = mx_kscale(D, 0)[:, None]
    return {
        "x": (n((G, D, N)) * s).astype(np.float32),
        "w": (n((G, D, M)) / np.sqrt(D) / s).astype(np.float32),
    }


def reference(x, w):
    xq = mxq(f64(x), 1, "e4m3")
    y = mxq(f64(w), 1, "e4m3").transpose(0, 2, 1) @ xq
    y = gelu(y)
    return y

@@ -1,0 +1,137 @@
+from contextlib import ExitStack
+
+import concourse.mybir as mybir
+
+G, D, M, N = 2, 256, 256, 1024
+FLOPS = 2 * G * D * M * N
+
+F32 = mybir.dt.float32
+BF16 = mybir.dt.bfloat16
+U32 = mybir.dt.uint32
+U8 = mybir.dt.uint8
+FP8X4 = mybir.dt.float8_e4m3fn_x4
+GELU = mybir.ActivationFunctionType.Gelu_apprx_tanh
+
+P = 128
+PACK = 4
+ROWS = D // PACK
+M_TILE = 128
+M_TILES = M // M_TILE
+SUB = 128
+BANK = 512
+LOADS = [256,256,256,256]
+STORES = [256,256,256,256]
+PIECE = 128
+BY_GROUP = False
+WARM = False
+RUN = 4
+
+
+def interleave(nc, dst, src):
+    nc.vector.tensor_copy(
+        out=dst.rearrange("p (c i) j -> p c j i", i=RUN),
+        in_=src.rearrange("p j (c i) -> p c j i", i=RUN),
+    )
+
+
+def quantise(nc, codes, scales, src):
+    nc.vector.quantize_mx(out=codes.bitcast(FP8X4), scales=scales, in_=src.rearrange("p c j -> p (c j)"))
+
+
+def tile_rows_glin_gelu_kernel(tc, x, w, out):
+    nc = tc.nc
+    x_rows = x.rearrange("g (p j) n -> (g p) j n", j=PACK)
+    w_rows = w.rearrange("g (p j) m -> (g p) j m", j=PACK)
+    out_rows = out.rearrange("g (t s) n -> s (g t) n", s=M_TILE)
+
+    with ExitStack() as ctx:
+        keep = ctx.enter_context(tc.tile_pool(name="keep", bufs=1))
+        psum = ctx.enter_context(tc.psum_pool(name="psum", bufs=1))
+        ctx.enter_context(tc.manual_schedule())
+
+        w_raw = keep.tile([P, PACK, M], F32, name="w_raw")
+        nc.sync.dma_start(out=w_raw[:], in_=w_rows)
+        x_raw = []
+        n0 = 0
+        for c, width in enumerate(LOADS):
+            raw = keep.tile([P, PACK, width], F32, name="x_raw%d" % c)
+            nc.sync.dma_start(out=raw[:], in_=x_rows[:, :, n0 : n0 + width])
+            x_raw.append((raw, n0, width))
+            n0 += width
+
+        if WARM:
+            zero = keep.tile([P, 8], F32, name="zero")
+            nc.gpsimd.memset(zero[:], 0.0)
+            warm = keep.tile([P, 8], F32, name="warm")
+            nc.scalar.activation(out=warm[:, 0:1], in_=zero[:, 0:1], func=GELU)
+
+        w_bf = [keep.tile([P, M_TILE, PACK], BF16, name="w_bf%d" % t, align_bytes=64) for t in range(M_TILES)]
+        w_codes = [keep.tile([P, M_TILE], U32, name="w_codes%d" % t, align_bytes=64) for t in range(M_TILES)]
+        w_scales = [keep.tile([P, M_TILE], U8, name="w_scales%d" % t, align_bytes=64) for t in range(M_TILES)]
+        for t in range(M_TILES):
+            interleave(nc, w_bf[t][:], w_raw[:, :, t * M_TILE : (t + 1) * M_TILE])
+        for t in range(M_TILES):
+            quantise(nc, w_codes[t][:], w_scales[t][:], w_bf[t][:])
+
+        banks = [[psum.tile([M_TILE, BANK], F32, name="bank%d_%d" % (g, b)) for b in range(4)] for g in range(G)]
+        subs = N // SUB
+        x_bf = [keep.tile([P, SUB, PACK], BF16, name="x_bf%d" % s, align_bytes=64) for s in range(subs)]
+        x_codes = [keep.tile([P, SUB], U32, name="x_codes%d" % s, align_bytes=64) for s in range(subs)]
+        x_scales = [keep.tile([P, SUB], U8, name="x_scales%d" % s, align_bytes=64) for s in range(subs)]
+
+        store_of = {}
+        results = []
+        n0 = 0
+        for k, width in enumerate(STORES):
+            res = keep.tile([P, G * M_TILES, width], F32, name="res%d" % k)
+            results.append((res, n0, width))
+            for s in range(n0 // SUB, (n0 + width) // SUB):
+                store_of[s] = k
+            n0 += width
+        done = set()
+
+        def sums(g, s):
+            half = (s // 4) * M_TILES * SUB
+            return banks[g][s % 4][:, half : half + M_TILES * SUB]
+
+        def gelu_and_store(g, s):
+            res, n0, width = results[store_of[s]]
+            lo = s * SUB - n0
+            nc.scalar.activation(
+                out=res[:, g * M_TILES : (g + 1) * M_TILES, lo : lo + SUB],
+                in_=sums(g, s).rearrange("p (t n) -> p t n", t=M_TILES),
+                func=GELU,
+            )
+            done.add((g, s))
+            mine = range(n0 // SUB, (n0 + width) // SUB)
+            if BY_GROUP:
+                if all((g, u) in done for u in mine):
+                    q = slice(g * M_TILES, (g + 1) * M_TILES)
+                    nc.sync.dma_start(out=out_rows[:, q, n0 : n0 + width], in_=res[:, q, :])
+            elif all((h, u) in done for u in mine for h in range(G)):
+                nc.sync.dma_start(out=out_rows[:, :, n0 : n0 + width], in_=res[:])
+
+        for raw, n0, width in x_raw:
+            mine = list(range(n0 // SUB, (n0 + width) // SUB))
+            pieces = [(s, lo) for s in mine for lo in range(0, SUB, PIECE)]
+            for s, lo in pieces:
+                a = s * SUB - n0 + lo
+                interleave(nc, x_bf[s][:, lo : lo + PIECE, :], raw[:, :, a : a + PIECE])
+            for s, lo in pieces:
+                quantise(nc, x_codes[s][:, lo : lo + PIECE], x_scales[s][:, lo : lo + PIECE], x_bf[s][:, lo : lo + PIECE, :])
+            for s in mine:
+                for t in range(M_TILES):
+                    for g in range(G):
+                        rows = slice(g * ROWS, (g + 1) * ROWS)
+                        nc.tensor.matmul_mx(
+                            out=sums(g, s)[:, t * SUB : (t + 1) * SUB],
+                            lhsT=w_codes[t][rows, :].bitcast(FP8X4),
+                            lhsT_scale=w_scales[t][rows, :],
+                            rhs=x_codes[s][rows, :].bitcast(FP8X4),
+                            rhs_scale=x_scales[s][rows, :],
+                            start=True,
+                            stop=True,
+                        )
+            order = [(g, s) for g in range(G) for s in mine] if BY_GROUP else [(g, s) for s in mine for g in range(G)]
+            for g, s in order:
+                gelu_and_store(g, s)

@@ -22,9 +22,9 @@ BANK = 512
 LOADS = [256,256,256,256]
 STORES = [256,256,256,256]
 PIECE = 128
-BY_GROUP = False
+BY_GROUP = True
 WARM = False
-RUN = 4
+RUN = 2
 
 
 def interleave(nc, dst, src):

from contextlib import ExitStack

import concourse.mybir as mybir

G, D, M, N = 2, 256, 256, 1024
FLOPS = 2 * G * D * M * N

F32 = mybir.dt.float32
BF16 = mybir.dt.bfloat16
U32 = mybir.dt.uint32
U8 = mybir.dt.uint8
FP8X4 = mybir.dt.float8_e4m3fn_x4
GELU = mybir.ActivationFunctionType.Gelu_apprx_tanh

P = 128
PACK = 4
ROWS = D // PACK
M_TILE = 128
M_TILES = M // M_TILE
SUB = 128
BANK = 512
LOADS = [256,256,256,256]
STORES = [256,256,256,256]
PIECE = 128
BY_GROUP = True
WARM = False
RUN = 2


def interleave(nc, dst, src):
    nc.vector.tensor_copy(
        out=dst.rearrange("p (c i) j -> p c j i", i=RUN),
        in_=src.rearrange("p j (c i) -> p c j i", i=RUN),
    )


def quantise(nc, codes, scales, src):
    nc.vector.quantize_mx(out=codes.bitcast(FP8X4), scales=scales, in_=src.rearrange("p c j -> p (c j)"))


def tile_rows_glin_gelu_kernel(tc, x, w, out):
    nc = tc.nc
    x_rows = x.rearrange("g (p j) n -> (g p) j n", j=PACK)
    w_rows = w.rearrange("g (p j) m -> (g p) j m", j=PACK)
    out_rows = out.rearrange("g (t s) n -> s (g t) n", s=M_TILE)

    with ExitStack() as ctx:
        keep = ctx.enter_context(tc.tile_pool(name="keep", bufs=1))
        psum = ctx.enter_context(tc.psum_pool(name="psum", bufs=1))
        ctx.enter_context(tc.manual_schedule())

        w_raw = keep.tile([P, PACK, M], F32, name="w_raw")
        nc.sync.dma_start(out=w_raw[:], in_=w_rows)
        x_raw = []
        n0 = 0
        for c, width in enumerate(LOADS):
            raw = keep.tile([P, PACK, width], F32, name="x_raw%d" % c)
            nc.sync.dma_start(out=raw[:], in_=x_rows[:, :, n0 : n0 + width])
            x_raw.append((raw, n0, width))
            n0 += width

        if WARM:
            zero = keep.tile([P, 8], F32, name="zero")
            nc.gpsimd.memset(zero[:], 0.0)
            warm = keep.tile([P, 8], F32, name="warm")
            nc.scalar.activation(out=warm[:, 0:1], in_=zero[:, 0:1], func=GELU)

        w_bf = [keep.tile([P, M_TILE, PACK], BF16, name="w_bf%d" % t, align_bytes=64) for t in range(M_TILES)]
        w_codes = [keep.tile([P, M_TILE], U32, name="w_codes%d" % t, align_bytes=64) for t in range(M_TILES)]
        w_scales = [keep.tile([P, M_TILE], U8, name="w_scales%d" % t, align_bytes=64) for t in range(M_TILES)]
        for t in range(M_TILES):
            interleave(nc, w_bf[t][:], w_raw[:, :, t * M_TILE : (t + 1) * M_TILE])
        for t in range(M_TILES):
            quantise(nc, w_codes[t][:], w_scales[t][:], w_bf[t][:])

        banks = [[psum.tile([M_TILE, BANK], F32, name="bank%d_%d" % (g, b)) for b in range(4)] for g in range(G)]
        subs = N // SUB
        x_bf = [keep.tile([P, SUB, PACK], BF16, name="x_bf%d" % s, align_bytes=64) for s in range(subs)]
        x_codes = [keep.tile([P, SUB], U32, name="x_codes%d" % s, align_bytes=64) for s in range(subs)]
        x_scales = [keep.tile([P, SUB], U8, name="x_scales%d" % s, align_bytes=64) for s in range(subs)]

        store_of = {}
        results = []
        n0 = 0
        for k, width in enumerate(STORES):
            res = keep.tile([P, G * M_TILES, width], F32, name="res%d" % k)
            results.append((res, n0, width))
            for s in range(n0 // SUB, (n0 + width) // SUB):
                store_of[s] = k
            n0 += width
        done = set()

        def sums(g, s):
            half = (s // 4) * M_TILES * SUB
            return banks[g][s % 4][:, half : half + M_TILES * SUB]

        def gelu_and_store(g, s):
            res, n0, width = results[store_of[s]]
            lo = s * SUB - n0
            nc.scalar.activation(
                out=res[:, g * M_TILES : (g + 1) * M_TILES, lo : lo + SUB],
                in_=sums(g, s).rearrange("p (t n) -> p t n", t=M_TILES),
                func=GELU,
            )
            done.add((g, s))
            mine = range(n0 // SUB, (n0 + width) // SUB)
            if BY_GROUP:
                if all((g, u) in done for u in mine):
                    q = slice(g * M_TILES, (g + 1) * M_TILES)
                    nc.sync.dma_start(out=out_rows[:, q, n0 : n0 + width], in_=res[:, q, :])
            elif all((h, u) in done for u in mine for h in range(G)):
                nc.sync.dma_start(out=out_rows[:, :, n0 : n0 + width], in_=res[:])

        for raw, n0, width in x_raw:
            mine = list(range(n0 // SUB, (n0 + width) // SUB))
            pieces = [(s, lo) for s in mine for lo in range(0, SUB, PIECE)]
            for s, lo in pieces:
                a = s * SUB - n0 + lo
                interleave(nc, x_bf[s][:, lo : lo + PIECE, :], raw[:, :, a : a + PIECE])
            for s, lo in pieces:
                quantise(nc, x_codes[s][:, lo : lo + PIECE], x_scales[s][:, lo : lo + PIECE], x_bf[s][:, lo : lo + PIECE, :])
            for s in mine:
                for t in range(M_TILES):
                    for g in range(G):
                        rows = slice(g * ROWS, (g + 1) * ROWS)
                        nc.tensor.matmul_mx(
                            out=sums(g, s)[:, t * SUB : (t + 1) * SUB],
                            lhsT=w_codes[t][rows, :].bitcast(FP8X4),
                            lhsT_scale=w_scales[t][rows, :],
                            rhs=x_codes[s][rows, :].bitcast(FP8X4),
                            rhs_scale=x_scales[s][rows, :],
                            start=True,
                            stop=True,
                        )
            order = [(g, s) for g in range(G) for s in mine] if BY_GROUP else [(g, s) for s in mine for g in range(G)]
            for g, s in order:
                gelu_and_store(g, s)
